import numpy as np
import ml_dtypes

BF16 = ml_dtypes.bfloat16


def bf(x):
    return np.asarray(x, np.float32).astype(BF16)


def f32(x):
    return np.asarray(x, np.float32)


def f64(x):
    return np.asarray(x).astype(np.float64)


def striped(idx):
    return np.tile(idx.reshape(-1, 16).T, (8, 1))


S, K, M, N, B, Q = 512, 128, 128, 256, 2, 128


def setup_inputs():
    return {"base": bf(np.random.standard_normal((B, M, S))), "x": bf(np.random.standard_normal((K, N))), "w": bf(np.random.standard_normal((K, M)) / np.sqrt(K)), "c": f32(0.2 + 0.8 * np.random.random_sample((1, S))), "offs": striped(np.random.permutation(S)[:N])}


def reference(base, x, w, c, offs):
    idx = offs[:16].T.reshape(-1)
    z = f64(base).copy()
    for i in range(B):
        z[i][:, idx[i * Q : (i + 1) * Q]] += f64(w).T @ f64(x)[:, i * Q : (i + 1) * Q]
    return z * f64(c)

@@ -1,0 +1,52 @@
+import concourse.mybir as mybir
+from concourse.masks import make_identity
+
+BF16, F32, U16 = mybir.dt.bfloat16, mybir.dt.float32, mybir.dt.uint16
+mult = mybir.AluOpType.mult
+
+SEQUENCES, P, TOKENS = 2, 128, 512
+PIECE = 128
+OFFSET_COLUMNS = PIECE // 16
+
+FLOPS = 2 * P * P * SEQUENCES * PIECE + P * SEQUENCES * PIECE + SEQUENCES * P * TOKENS
+
+
+def tile_scatter_matmul_kernel(tc, base, x, w, c, offs, out):
+    nc = tc.nc
+    with (
+        tc.tile_pool(name="held", bufs=1) as held,
+        tc.psum_pool(name="psum", bufs=1) as psum,
+    ):
+        base_tile = held.tile([P, SEQUENCES, TOKENS], BF16)
+        w_tile = held.tile([P, P], BF16)
+        x_tile = held.tile([P, SEQUENCES * PIECE], BF16)
+        offsets = held.tile([P, SEQUENCES * OFFSET_COLUMNS], U16)
+        c_tile = held.tile([P, TOKENS], F32)
+
+        nc.sync.dma_start(base_tile[:], base.rearrange("b m t -> m b t"))
+        nc.sync.dma_start(w_tile[:], w)
+        nc.sync.dma_start(x_tile[:], x)
+        nc.sync.dma_start(offsets[:], offs)
+        nc.sync.dma_start(c_tile[:], c.rearrange("o t -> (o t)").partition_broadcast(P))
+
+        identity = held.tile([P, P], BF16)
+        make_identity(nc, identity[:])
+
+        windows = [psum.tile([P, TOKENS], F32, name=f"window{i}") for i in range(SEQUENCES)]
+        for i in range(SEQUENCES):
+            nc.tensor.matmul(windows[i][:], identity[:], base_tile[:, i, :], start=True, stop=False)
+
+        for i in range(SEQUENCES):
+            piece = offsets[:, i * OFFSET_COLUMNS : (i + 1) * OFFSET_COLUMNS]
+            nc.tensor.matmul(
+                windows[i][:].indirect(piece),
+                w_tile[:],
+                x_tile[:, i * PIECE : (i + 1) * PIECE],
+                start=False,
+                stop=True,
+            )
+
+        for i in range(SEQUENCES):
+            scaled = held.tile([P, TOKENS], F32, name=f"scaled{i}")
+            nc.vector.tensor_tensor(scaled[:], windows[i][:], c_tile[:], mult)
+            nc.sync.dma_start(out[i], scaled[:])

@@ -21,18 +21,25 @@ def tile_scatter_matmul_kernel(tc, base, x, w, c, offs, out):
         w_tile = held.tile([P, P], BF16)
         x_tile = held.tile([P, SEQUENCES * PIECE], BF16)
         offsets = held.tile([P, SEQUENCES * OFFSET_COLUMNS], U16)
+        c_row = held.tile([1, TOKENS], F32)
         c_tile = held.tile([P, TOKENS], F32)
+        ones = held.tile([1, P], F32)
+        identity = held.tile([P, P], BF16)
+        windows = [psum.tile([P, TOKENS], F32, name=f"window{i}") for i in range(SEQUENCES)]
+        c_bank = psum.tile([P, TOKENS], F32)
 
         nc.sync.dma_start(base_tile[:], base.rearrange("b m t -> m b t"))
         nc.sync.dma_start(w_tile[:], w)
         nc.sync.dma_start(x_tile[:], x)
         nc.sync.dma_start(offsets[:], offs)
-        nc.sync.dma_start(c_tile[:], c.rearrange("o t -> (o t)").partition_broadcast(P))
+        nc.scalar.dma_start(c_row[:], c)
 
-        identity = held.tile([P, P], BF16)
+        nc.vector.memset(ones[:], 1.0)
         make_identity(nc, identity[:])
 
-        windows = [psum.tile([P, TOKENS], F32, name=f"window{i}") for i in range(SEQUENCES)]
+        nc.tensor.matmul(c_bank[:], ones[:], c_row[:], start=True, stop=True)
+        nc.vector.tensor_copy(c_tile[:], c_bank[:])
+
         for i in range(SEQUENCES):
             nc.tensor.matmul(windows[i][:], identity[:], base_tile[:, i, :], start=True, stop=False)
 

@@ -8,6 +8,8 @@ SEQUENCES, P, TOKENS = 2, 128, 512
 PIECE = 128
 OFFSET_COLUMNS = PIECE // 16
 
+WARM_UPS = 16
+
 FLOPS = 2 * P * P * SEQUENCES * PIECE + P * SEQUENCES * PIECE + SEQUENCES * P * TOKENS
 
 
@@ -24,18 +26,24 @@ def tile_scatter_matmul_kernel(tc, base, x, w, c, offs, out):
         c_row = held.tile([1, TOKENS], F32)
         c_tile = held.tile([P, TOKENS], F32)
         ones = held.tile([1, P], F32)
+        zeros = held.tile([P, P], BF16)
         identity = held.tile([P, P], BF16)
         windows = [psum.tile([P, TOKENS], F32, name=f"window{i}") for i in range(SEQUENCES)]
         c_bank = psum.tile([P, TOKENS], F32)
+        spare = psum.tile([P, P], F32)
 
+        nc.sync.dma_start(c_row[:], c)
         nc.sync.dma_start(base_tile[:], base.rearrange("b m t -> m b t"))
         nc.sync.dma_start(w_tile[:], w)
         nc.sync.dma_start(x_tile[:], x)
         nc.sync.dma_start(offsets[:], offs)
-        nc.scalar.dma_start(c_row[:], c)
 
+        nc.gpsimd.memset(zeros[:], 0.0)
         nc.vector.memset(ones[:], 1.0)
         make_identity(nc, identity[:])
+
+        for repeat in range(WARM_UPS):
+            nc.tensor.matmul(spare[:], zeros[:], zeros[:], start=True, stop=True)
 
         nc.tensor.matmul(c_bank[:], ones[:], c_row[:], start=True, stop=True)
         nc.vector.tensor_copy(c_tile[:], c_bank[:])

import concourse.mybir as mybir
from concourse.masks import make_identity

BF16, F32, U16 = mybir.dt.bfloat16, mybir.dt.float32, mybir.dt.uint16
mult = mybir.AluOpType.mult

SEQUENCES, P, TOKENS = 2, 128, 512
PIECE = 128
OFFSET_COLUMNS = PIECE // 16

WARM_UPS = 16

FLOPS = 2 * P * P * SEQUENCES * PIECE + P * SEQUENCES * PIECE + SEQUENCES * P * TOKENS


def tile_scatter_matmul_kernel(tc, base, x, w, c, offs, out):
    nc = tc.nc
    with (
        tc.tile_pool(name="held", bufs=1) as held,
        tc.psum_pool(name="psum", bufs=1) as psum,
    ):
        base_tile = held.tile([P, SEQUENCES, TOKENS], BF16)
        w_tile = held.tile([P, P], BF16)
        x_tile = held.tile([P, SEQUENCES * PIECE], BF16)
        offsets = held.tile([P, SEQUENCES * OFFSET_COLUMNS], U16)
        c_row = held.tile([1, TOKENS], F32)
        c_tile = held.tile([P, TOKENS], F32)
        ones = held.tile([1, P], F32)
        zeros = held.tile([P, P], BF16)
        identity = held.tile([P, P], BF16)
        windows = [psum.tile([P, TOKENS], F32, name=f"window{i}") for i in range(SEQUENCES)]
        c_bank = psum.tile([P, TOKENS], F32)
        spare = psum.tile([P, P], F32)

        nc.sync.dma_start(c_row[:], c)
        nc.sync.dma_start(base_tile[:], base.rearrange("b m t -> m b t"))
        nc.sync.dma_start(w_tile[:], w)
        nc.sync.dma_start(x_tile[:], x)
        nc.sync.dma_start(offsets[:], offs)

        nc.gpsimd.memset(zeros[:], 0.0)
        nc.vector.memset(ones[:], 1.0)
        make_identity(nc, identity[:])

        for repeat in range(WARM_UPS):
            nc.tensor.matmul(spare[:], zeros[:], zeros[:], start=True, stop=True)

        nc.tensor.matmul(c_bank[:], ones[:], c_row[:], start=True, stop=True)
        nc.vector.tensor_copy(c_tile[:], c_bank[:])

        for i in range(SEQUENCES):
            nc.tensor.matmul(windows[i][:], identity[:], base_tile[:, i, :], start=True, stop=False)

        for i in range(SEQUENCES):
            piece = offsets[:, i * OFFSET_COLUMNS : (i + 1) * OFFSET_COLUMNS]
            nc.tensor.matmul(
                windows[i][:].indirect(piece),
                w_tile[:],
                x_tile[:, i * PIECE : (i + 1) * PIECE],
                start=False,
                stop=True,
            )

        for i in range(SEQUENCES):
            scaled = held.tile([P, TOKENS], F32, name=f"scaled{i}")
            nc.vector.tensor_tensor(scaled[:], windows[i][:], c_tile[:], mult)
            nc.sync.dma_start(out[i], scaled[:])
